import numpy as np
import ml_dtypes


def mxq(x, axis, fmt="e4m3"):
    dtype, down = {"e4m3": (ml_dtypes.float8_e4m3fn, 7), "e5m2": (ml_dtypes.float8_e5m2, 14)}[fmt]
    v = np.moveaxis(np.asarray(x, np.float32).astype(ml_dtypes.bfloat16).astype(np.float64), axis, -1)
    blocks = v.reshape(v.shape[:-1] + (-1, 32))
    amax = np.abs(blocks).max(-1, keepdims=True)
    byte = np.maximum(np.where(amax > 0, np.frexp(amax)[1] - 1 + 127, 0) - down, 1)
    scale = np.exp2(byte - 127.0)
    codes = (blocks / scale).astype(np.float32).astype(dtype).astype(np.float64)
    return np.moveaxis((codes * scale).reshape(v.shape), -1, axis)


WIDE = False


def mx_kscale(k):
    if not WIDE:
        return np.ones(k)
    levels = np.array([10, -10, 5, -5, 0])
    if k % 512:
        return np.exp2(np.random.permutation(np.resize(levels, k // 32))).repeat(32)
    a = np.empty((k // 512, 16))
    for p in range(k // 512):
        a[p, :8] = np.random.permutation(np.resize(levels, 8))
        for g in range(8):
            far = levels[np.abs(levels - a[p, g]) >= 10]
            a[p, g + 8] = far[np.random.randint(len(far))]
    return np.exp2(a.ravel()).repeat(32)


def f64(x):
    return np.asarray(x).astype(np.float64)


def striped(idx):
    return np.tile(idx.reshape(-1, 16).T, (8, 1)).astype(np.uint16)


def unstriped(offs):
    return offs[:16].T.reshape(-1).astype(np.int64)


E2M1 = np.array([0.0, 0.5, 1.0, 1.5, 2.0, 3.0, 4.0, 6.0, -0.0, -0.5, -1.0, -1.5, -2.0, -3.0, -4.0, -6.0])


def pack_weight(w, fmt):
    k, n = w.shape
    w = f64(np.asarray(w, np.float32).astype(ml_dtypes.bfloat16)).reshape(k // 32, 32, n)
    amax = np.abs(w).max(1)
    if fmt == "e4m3":
        byte = np.frexp(amax)[1] - 1 + 127 - 7
    else:
        mant, ex = np.frexp(amax / 6.0)
        byte = np.where(mant > 0.5, ex, ex - 1) + 127
    byte = np.clip(np.where(amax > 0, byte, 1), 1, 254)
    scaled = (w * np.exp2(127.0 - byte)[:, None, :]).reshape(k, n).astype(np.float32)
    by_word = np.ascontiguousarray(scaled.reshape(k // 512, 128, 4, n).transpose(0, 1, 3, 2))
    if fmt == "e4m3":
        words = by_word.astype(ml_dtypes.float8_e4m3fn).view(np.uint8)
    else:
        c = by_word.astype(ml_dtypes.float4_e2m1fn).view(np.uint8) & 0xF
        words = (c[..., 0::2] | (c[..., 1::2] << 4)).reshape(k // 512, 128, 2 * n)
    return np.ascontiguousarray(words), np.ascontiguousarray(byte.astype(np.uint8).reshape(k // 512, 16, n))


def unpack_weight(words, scales, fmt):
    g, _, n = scales.shape
    words = np.ascontiguousarray(words).reshape(g, 128, n, -1)
    if fmt == "e4m3":
        vals = words.view(ml_dtypes.float8_e4m3fn).astype(np.float64)
    else:
        nib = np.empty((g, 128, n, 4), np.uint8)
        nib[..., 0::2] = words & 0xF
        nib[..., 1::2] = words >> 4
        vals = E2M1[nib]
    vals = vals * np.repeat(np.exp2(scales.astype(np.float64) - 127.0), 8, axis=1)[..., None]
    return vals.transpose(0, 1, 3, 2).reshape(g * 512, n)


def gelu(v):
    return 0.5 * v * (1.0 + np.tanh(np.sqrt(2.0 / np.pi) * (v + 0.044715 * v**3)))


K, H, T, S, T2, S2, T3, P = 1024, 1024, 2048, 512, 1024, 1024, 2048, 512


def setup_inputs():
    n = np.random.standard_normal
    s = mx_kscale(K)[:, None]
    u = mx_kscale(H)[:, None]
    tab_words, tab_scales = pack_weight(n((K, T)) * s, "e4m3")
    tab2_words, tab2_scales = pack_weight(n((H, T3)) / u / np.sqrt(H), "e4m3")
    w4_words, w4_scales = pack_weight(n((K, H)) / s / np.sqrt(K), "e2m1")
    return {
        "tab_words": tab_words, "tab_scales": tab_scales,
        "offs": striped(np.random.permutation(T)[:S]),
        "tab2_words": tab2_words, "tab2_scales": tab2_scales,
        "offs2": striped(np.random.permutation(T3)[:S2]),
        "offs3": striped(np.random.permutation(T2)[:S]),
        "offs4": striped(np.random.permutation(T2)[:P]),
        "w1": (n((K, H)) / s / np.sqrt(K)).astype(np.float32),
        "w4_words": w4_words, "w4_scales": w4_scales,
        "gain": (np.exp(0.3 * n(H)) * u[:, 0]).astype(np.float32),
        "wgs": np.exp(0.3 * n((128, S))).astype(np.float32),
        "page0": (n((H, T2)) * u).astype(np.float32),
        "base": (0.6 * n(H) * u[:, 0]).astype(np.float32),
    }


def reference(tab_words, tab_scales, offs, tab2_words, tab2_scales, offs2, offs3, offs4,
              w1, w4_words, w4_scales, gain, wgs, page0, base):
    v = unpack_weight(tab_words, tab_scales, "e4m3")[:, unstriped(offs)]
    v2 = unpack_weight(tab2_words, tab2_scales, "e4m3")[:, unstriped(offs2)]
    a = mxq(f64(w1), 0, "e4m3").T @ v
    b = unpack_weight(w4_words, w4_scales, "e2m1").T @ v
    h = f64(gain)[:, None] * (np.abs(a) - np.abs(b))
    page = f64(page0).copy()
    page[:, unstriped(offs3)] = np.tile(f64(wgs), (H // 128, 1)) * h
    x = page[:, unstriped(offs4)]
    e1 = v2.T @ mxq(np.abs(x), 0, "e4m3")
    e2 = v2.T @ mxq(np.maximum(x, f64(base)[:, None]), 0, "e4m3")
    return np.maximum(e1, e2)

@@ -1,0 +1,376 @@
+from contextlib import ExitStack
+
+import concourse.mybir as mybir
+
+K, H, T, S, T2, S2, T3, PJ = 1024, 1024, 2048, 512, 1024, 1024, 2048, 512
+FLOPS = 2 * 2 * K * H * S + 2 * 2 * H * S2 * PJ
+
+F32 = mybir.dt.float32
+BF16 = mybir.dt.bfloat16
+I32 = mybir.dt.int32
+U32 = mybir.dt.uint32
+U16 = mybir.dt.uint16
+U8 = mybir.dt.uint8
+FP8X4 = mybir.dt.float8_e4m3fn_x4
+FP4X4 = mybir.dt.float4_e2m1fn_x4
+ALU = mybir.AluOpType
+ACT = mybir.ActivationFunctionType
+
+P = 128
+PACK = 4
+PASS = P * PACK
+NPASS = 2
+
+
+def tile_list_parish_record_hints_kernel(
+    tc, tab_words, tab_scales, offs, tab2_words, tab2_scales, offs2, offs3, offs4,
+    w1, w4_words, w4_scales, gain, wgs, page0, base, out,
+):
+    nc = tc.nc
+    with ExitStack() as ctx:
+        held = ctx.enter_context(tc.tile_pool(name="held", bufs=1))
+        shared = ctx.enter_context(tc.tile_pool(name="shared", bufs=1))
+        psum = ctx.enter_context(tc.psum_pool(name="psum", bufs=1))
+
+        def keep(name, shape, dtype):
+            return held.tile(shape, dtype, name=name, align_bytes=64)
+
+        o1 = keep("o1", [P, S // 16], U16)
+        o2 = keep("o2", [P, S2 // 16], U16)
+        o3 = keep("o3", [P, S // 16], U16)
+        o4 = keep("o4", [P, PJ // 16], U16)
+
+        tab_s = keep("tab_s", [P, NPASS * T], U8)
+        w4_s = keep("w4_s", [P, NPASS * H], U8)
+        tab2_s = keep("tab2_s", [P, T3], U8)
+        nc.vector.memset(tab_s[:].bitcast(I32), 0)
+        nc.gpsimd.memset(w4_s[:].bitcast(I32), 0)
+        nc.vector.memset(tab2_s[:].bitcast(I32), 0)
+
+        def load_planes(queue, tile, scales):
+            for q in range(4):
+                queue.dma_start(
+                    out=tile[32 * q : 32 * q + 4, :].bitcast(I32).rearrange("r (a t) -> r a t", a=NPASS),
+                    in_=scales[:, 4 * q : 4 * q + 4, :].bitcast(I32).rearrange("a r t -> r a t"),
+                )
+
+        def load_words(name, words, a):
+            tile = keep(name, [P, words.shape[2]], I32)
+            nc.sync.dma_start(out=tile[:], in_=words[a].rearrange("p t i -> p (t i)").bitcast(I32))
+            return tile
+
+        def load_w1(b, a):
+            raw = keep("raw%d" % a if b == 1 else "wide%d" % a, [P, PACK, PASS], F32)
+            nc.sync.dma_start(
+                out=raw[:],
+                in_=w1[PASS * a : PASS * (a + 1), PASS * b : PASS * (b + 1)].rearrange("(p i) c -> p i c", i=PACK),
+            )
+            return raw
+
+        def load_page(s):
+            b, t = divmod(s, PACK)
+            page = keep("page%d" % s, [P, T2], F32)
+            nc.sync.dma_start(
+                out=page[:], in_=page0[PASS * b : PASS * (b + 1), :].rearrange("(p t) c -> p t c", t=PACK)[:, t, :]
+            )
+            return page
+
+        nc.sync.dma_start(o1[:], offs)
+        nc.sync.dma_start(o2[:], offs2)
+        nc.sync.dma_start(o3[:], offs3)
+        nc.sync.dma_start(o4[:], offs4)
+        gain_t = keep("gain_t", [P, NPASS, PACK], F32)
+        nc.sync.dma_start(out=gain_t[:], in_=gain.rearrange("(b p t) -> p b t", b=NPASS, t=PACK))
+        base_t = keep("base_t", [P, NPASS, PACK], F32)
+        nc.sync.dma_start(out=base_t[:], in_=base.rearrange("(b p t) -> p b t", b=NPASS, t=PACK))
+
+        def load_w4(b):
+            raw = keep("w4_raw%d" % b, [P, NPASS * 2 * PASS], U8)
+            nc.sync.dma_start(
+                out=raw[:].bitcast(I32).rearrange("p (a c) -> p a c", a=NPASS),
+                in_=w4_words[:, :, 2 * PASS * b : 2 * PASS * (b + 1)].bitcast(I32).rearrange("a p c -> p a c"),
+            )
+            return raw
+
+        w4_raw = [load_w4(0)]
+        tab_w = [load_words("words0", tab_words, 0)]
+        load_planes(nc.sync, tab_s, tab_scales)
+        w1_raw = {(0, 0): load_w1(0, 0)}
+        load_planes(nc.sync, w4_s, w4_scales)
+        tab_w.append(load_words("words1", tab_words, 1))
+        w1_raw[(0, 1)] = load_w1(0, 1)
+        wgs_t = keep("wgs_t", [P, PACK * S], F32)
+
+        def load_wgs(lo, hi):
+            for q in range(4):
+                nc.sync.dma_start(
+                    out=wgs_t[32 * q : 32 * q + 32, S * lo : S * hi],
+                    in_=wgs.rearrange("(q t) j -> q (t j)", t=PACK)[:, S * lo : S * hi],
+                )
+
+        load_wgs(0, 2)
+        pages = [load_page(0)]
+        w4_raw.append(load_w4(1))
+        pages.append(load_page(1))
+        w1_raw[(1, 0)] = load_w1(1, 0)
+        load_wgs(2, PACK)
+        w1_raw[(1, 1)] = load_w1(1, 1)
+        pages.append(load_page(2))
+        pages.append(load_page(3))
+        for q in range(4):
+            nc.sync.dma_start(
+                out=tab2_s[32 * q : 32 * q + 4 * NPASS, :].bitcast(I32),
+                in_=tab2_scales[:, 4 * q : 4 * q + 4, :].bitcast(I32),
+            )
+
+        w4_w, w4_p = {}, {}
+
+        def deal_w4_words(b, tile):
+            w4_w[b] = tile
+            nc.vector.tensor_copy(
+                out=tile[:].bitcast(U16).rearrange("p (a t m) -> p a m t", t=PACK, m=P),
+                in_=w4_raw[b][:].bitcast(U16).rearrange("p (a m t) -> p a m t", t=PACK, m=P),
+            )
+
+        deal_w4_words(0, keep("w4_w0", [P, NPASS * 2 * PASS], U8))
+        v_w, v_s = [], []
+        for a in range(NPASS):
+            words = keep("v_w%d" % a, [P, S], U32)
+            plane = keep("v_s%d" % a, [P, S], U8)
+            nc.vector.tensor_copy(words[:], tab_w[a][:].bitcast(U32).indirect(o1[:]))
+            nc.vector.tensor_copy(plane[:], tab_s[:, T * a : T * (a + 1)].indirect(o1[:]))
+            v_w.append(words)
+            v_s.append(plane)
+
+        def deal_w4_planes(b, tile):
+            w4_p[b] = tile
+            nc.vector.tensor_copy(
+                out=tile[:].rearrange("p (a t m) -> p a m t", a=NPASS, t=PACK, m=P),
+                in_=w4_s[:].rearrange("p (a b m t) -> p b a m t", a=NPASS, t=PACK, m=P)[:, b],
+            )
+
+        deal_w4_planes(0, keep("w4_p0", [P, NPASS * PASS], U8))
+        tab2_w = [load_words("words%d" % a, tab2_words, a) for a in range(NPASS)]
+        for s in range(PACK, 2 * PACK):
+            pages.append(load_page(s))
+        minus_base = keep("minus_base", [P, NPASS, PACK], F32)
+        nc.scalar.activation(out=minus_base[:], in_=base_t[:], func=ACT.Copy, scale=-1.0)
+
+        w1_w, w1_s = {}, {}
+
+        w1_g = {}
+
+        def weave_w1(b, a, scalar_share, grouped):
+            w1_g[(b, a)] = grouped
+            dst = grouped.rearrange("p (t m i) -> p m i t", t=PACK, i=PACK)
+            src = w1_raw[(b, a)][:].rearrange("p i (m t) -> p m i t", t=PACK)
+            if scalar_share:
+                nc.scalar.activation(out=dst, in_=src, func=ACT.Copy)
+            else:
+                nc.vector.tensor_copy(out=dst, in_=src)
+
+        def quantise_w1(b, a, cuts):
+            grouped = w1_g[(b, a)]
+            w1_w[(b, a)] = keep("w1_w%d%d" % (b, a), [P, PASS], U32)
+            w1_s[(b, a)] = keep("w1_s%d%d" % (b, a), [P, PASS], U8)
+            for lo, hi in zip(cuts, cuts[1:]):
+                nc.vector.quantize_mx(
+                    out=w1_w[(b, a)][:, lo:hi].bitcast(FP8X4), scales=w1_s[(b, a)][:, lo:hi],
+                    in_=grouped[:, PACK * lo : PACK * hi],
+                )
+
+        work = [held.tile([P, 2, 2, S], F32, name="work%d" % u, align_bytes=64) for u in range(PACK)]
+        factor = {}
+
+        def make_factor(s, place):
+            b, t = divmod(s, PACK)
+            factor[s] = place
+            nc.scalar.activation(
+                out=place, in_=wgs_t[:, S * t : S * (t + 1)], func=ACT.Copy, scale=gain_t[:, b, t : t + 1]
+            )
+
+        def first_stage(s):
+            b, t = divmod(s, PACK)
+            u, h = divmod(s, 2)
+            swap = t // 2
+            acc_b = psum.tile([P, S], F32, name="bank%d" % (PACK * b + 2 * h + swap))
+            acc_a = psum.tile([P, S], F32, name="bank%d" % (PACK * b + 2 * h + 1 - swap))
+            for a in range(NPASS):
+                c0 = PASS * a + P * t
+                nc.tensor.matmul_mx(
+                    out=acc_b[:],
+                    lhsT=w4_w[b][:, 2 * c0 : 2 * (c0 + P)].bitcast(FP4X4),
+                    lhsT_scale=w4_p[b][:, c0 : c0 + P],
+                    rhs=v_w[a][:].bitcast(FP8X4), rhs_scale=v_s[a][:],
+                    start=(a == 0), stop=(a == NPASS - 1),
+                )
+            for a in range(NPASS):
+                nc.tensor.matmul_mx(
+                    out=acc_a[:],
+                    lhsT=w1_w[(b, a)][:, P * t : P * (t + 1)].bitcast(FP8X4),
+                    lhsT_scale=w1_s[(b, a)][:, P * t : P * (t + 1)],
+                    rhs=v_w[a][:].bitcast(FP8X4), rhs_scale=v_s[a][:],
+                    start=(a == 0), stop=(a == NPASS - 1),
+                )
+            nc.scalar.activation(out=work[u][:, h, 1, :], in_=acc_b[:], func=ACT.Abs)
+            nc.scalar.activation(out=work[u][:, h, 0, :], in_=acc_a[:], func=ACT.Abs)
+
+        for a, share, cuts in ((0, P, (0, PASS)), (1, 0, (0, P, PASS))):
+            fresh = shared.tile([P, PACK * PASS], BF16, name="grouped%d" % a, offset=2 * PACK * PASS * a, align_bytes=64)
+            weave_w1(0, a, share, fresh[:])
+            quantise_w1(0, a, cuts)
+        for s in range(PACK):
+            first_stage(s)
+
+        deal_w4_words(1, shared.tile([P, NPASS * 2 * PASS], U8, name="w4_w1", offset=2 * PACK * PASS, align_bytes=64))
+        deal_w4_planes(1, shared.tile([P, NPASS * PASS], U8, name="w4_p1", offset=3 * PACK * PASS, align_bytes=64))
+
+        def as_bf16(pair):
+            return pair.rearrange("p h s -> p (h s)").bitcast(BF16)
+
+        x4, m4 = {}, {}
+
+        def subtract(u, part):
+            nc.vector.tensor_tensor(work[u][:, part, 0, :], work[u][:, part, 0, :], work[u][:, part, 1, :], ALU.subtract)
+
+        def scatter(s):
+            u, h = divmod(s, 2)
+            nc.vector.tensor_tensor(pages[s][:].indirect(o3[:]), work[u][:, h, 0, :], factor[s], ALU.mult)
+
+        def fetch(s):
+            b, t = divmod(s, PACK)
+            if t == 0:
+                x4[b] = keep("wide%d" % b, [P, PACK, PJ], F32)
+                m4[b] = keep("raw%d" % (1 - b), [P, PACK, PJ], F32)
+            nc.vector.tensor_copy(x4[b][:, t, :], pages[s][:].indirect(o4[:]))
+
+        def floor_on_scalar(s):
+            b, t = divmod(s, PACK)
+            above = m4[b][:, t, :]
+            nc.scalar.activation(out=above, in_=x4[b][:, t, :], func=ACT.Relu, bias=minus_base[:, b, t : t + 1])
+            nc.scalar.activation(out=m4[b][:, t, :], in_=above, func=ACT.Identity, bias=base_t[:, b, t : t + 1])
+
+        def floor_on_vector(s):
+            b, t = divmod(s, PACK)
+            nc.vector.tensor_scalar(m4[b][:, t, :], x4[b][:, t, :], base_t[:, b, t : t + 1], None, ALU.max)
+
+        x_w, x_s, x_g = {}, {}, {}
+
+        def weave(e, b, on_vector=False):
+            grouped = keep("x_g%d%d" % (e, b), [P, PJ, PACK], BF16)
+            dst = grouped[:].rearrange("p (c i) t -> p c t i", i=4)
+            src = (x4, m4)[e][b][:].rearrange("p t (c i) -> p c t i", i=4)
+            if on_vector:
+                nc.vector.tensor_copy(out=dst, in_=src)
+            else:
+                nc.scalar.activation(out=dst, in_=src, func=(ACT.Abs, ACT.Copy)[e])
+            x_g[(e, b)] = grouped
+
+        def quantise_x(e, b):
+            x_w[(e, b)] = keep("x_w%d%d" % (e, b), [P, PJ], U32)
+            x_s[(e, b)] = keep("x_s%d%d" % (e, b), [P, PJ], U8)
+            nc.vector.quantize_mx(
+                out=x_w[(e, b)][:].bitcast(FP8X4), scales=x_s[(e, b)][:],
+                in_=x_g[(e, b)][:].rearrange("p j t -> p (j t)"),
+            )
+
+        half = S2 // 2
+        v2_s = keep("v2_s", [P, S2], U8)
+        v2_w = {}
+
+        def gather_records(g, name):
+            part = o2[:, (half // 16) * g : (half // 16) * (g + 1)]
+            v2_w[g] = keep(name, [P, NPASS, half], U32)
+            for a in range(NPASS):
+                nc.vector.tensor_copy(v2_w[g][:, a, :], tab2_w[a][:].bitcast(U32).indirect(part))
+
+        accs = {}
+
+        def bank_of(mt, e):
+            if mt < PACK:
+                return 2 * mt + e
+            late = 2 * (mt - PACK) + (1 - e)
+            return 2 * (late % PACK) + (1 - late // PACK)
+
+        def second_stage(mt, e, a):
+            g, c0 = divmod(P * mt, half)
+            if a == 0:
+                accs[(mt, e)] = psum.tile([P, PJ], F32, name="bank%d" % bank_of(mt, e))
+            nc.tensor.matmul_mx(
+                out=accs[(mt, e)][:],
+                lhsT=v2_w[g][:, a, c0 : c0 + P].bitcast(FP8X4),
+                lhsT_scale=v2_s[4 * a : P, P * mt : P * (mt + 1)],
+                rhs=x_w[(e, a)][:].bitcast(FP8X4), rhs_scale=x_s[(e, a)][:],
+                start=(a == 0), stop=(a == NPASS - 1),
+            )
+
+        def copy_out(mt):
+            u, h = divmod(mt, 2)
+            nc.scalar.copy(out=work[u][:, h, 0, :], in_=accs[(mt, 1)][:])
+
+        def finish(mt):
+            u, h = divmod(mt, 2)
+            nc.vector.tensor_tensor(work[u][:, h, 1, :], accs[(mt, 0)][:], work[u][:, h, 0, :], ALU.max)
+            nc.sync.dma_start(out=out[P * mt : P * (mt + 1), :], in_=work[u][:, h, 1, :])
+
+        subtract(0, slice(0, 1))
+        first_factors = keep("first_factors", [P, 2, S], F32)
+        make_factor(0, first_factors[:, 0, :])
+        make_factor(1, first_factors[:, 1, :])
+        scatter(0)
+        subtract(0, slice(1, 2))
+        weave_w1(1, 0, P, as_bf16(work[0][:, 0]))
+        scatter(1)
+        weave_w1(1, 1, P, as_bf16(work[0][:, 1]))
+        for u in range(PACK - 1):
+            if u > 0:
+                scatter(2 * u)
+                scatter(2 * u + 1)
+            subtract(u + 1, slice(0, 2))
+            make_factor(2 * u + 2, work[u + 1][:, 0, 1, :])
+            if u < PACK - 2:
+                make_factor(2 * u + 3, work[u + 1][:, 1, 1, :])
+            fetch(2 * u)
+            fetch(2 * u + 1)
+            if u == 0:
+                quantise_w1(1, 0, (0, PASS))
+                quantise_w1(1, 1, (0, PASS))
+                for s in range(PACK, 2 * PACK):
+                    first_stage(s)
+            floor_on_scalar(2 * u)
+            floor_on_scalar(2 * u + 1)
+            if u == 1:
+                weave(0, 0)
+                weave(1, 0)
+        scatter(6)
+        nc.vector.tensor_copy(v2_s[:], tab2_s[:].indirect(o2[:]))
+        for e in range(2):
+            quantise_x(e, 0)
+        make_factor(7, x_g[(1, 0)][:].rearrange("p j t -> p (j t)").bitcast(F32)[:, :S])
+        gather_records(0, "x_g00")
+        for mt in range(PACK):
+            for e in range(2):
+                second_stage(mt, e, 0)
+        scatter(7)
+        fetch(6)
+        fetch(7)
+        floor_on_scalar(6)
+        floor_on_vector(2 * PACK - 1)
+        weave(0, 1)
+        weave(1, 1, on_vector=True)
+        quantise_x(1, 1)
+        quantise_x(0, 1)
+        gather_records(1, "x_g11")
+        for e in (1, 0):
+            for mt in range(PACK):
+                second_stage(mt, e, 1)
+        for mt in range(PACK):
+            copy_out(mt)
+        for mt in range(PACK):
+            finish(mt)
+        for mt in range(PACK, 2 * PACK):
+            for e in (1, 0):
+                for a in range(NPASS):
+                    second_stage(mt, e, a)
+            copy_out(mt)
+            finish(mt)

@@ -1,6 +1,7 @@
 from contextlib import ExitStack
 
 import concourse.mybir as mybir
+from concourse.masks import make_identity
 
 K, H, T, S, T2, S2, T3, PJ = 1024, 1024, 2048, 512, 1024, 1024, 2048, 512
 FLOPS = 2 * 2 * K * H * S + 2 * 2 * H * S2 * PJ
@@ -30,6 +31,7 @@ def tile_list_parish_record_hints_kernel(
     with ExitStack() as ctx:
         held = ctx.enter_context(tc.tile_pool(name="held", bufs=1))
         shared = ctx.enter_context(tc.tile_pool(name="shared", bufs=1))
+        ring = ctx.enter_context(tc.tile_pool(name="ring", bufs=4))
         psum = ctx.enter_context(tc.psum_pool(name="psum", bufs=1))
 
         def keep(name, shape, dtype):
@@ -45,7 +47,6 @@ def tile_list_parish_record_hints_kernel(
         tab2_s = keep("tab2_s", [P, T3], U8)
         nc.vector.memset(tab_s[:].bitcast(I32), 0)
         nc.gpsimd.memset(w4_s[:].bitcast(I32), 0)
-        nc.vector.memset(tab2_s[:].bitcast(I32), 0)
 
         def load_planes(queue, tile, scales):
             for q in range(4):
@@ -53,6 +54,11 @@ def tile_list_parish_record_hints_kernel(
                     out=tile[32 * q : 32 * q + 4, :].bitcast(I32).rearrange("r (a t) -> r a t", a=NPASS),
                     in_=scales[:, 4 * q : 4 * q + 4, :].bitcast(I32).rearrange("a r t -> r a t"),
                 )
+
+        load_planes(nc.gpsimd, w4_s, w4_scales)
+        nc.gpsimd.memset(tab2_s[:].bitcast(I32), 0)
+        ident = keep("ident", [P, P], F32)
+        make_identity(nc, ident[:])
 
         def load_words(name, words, a):
             tile = keep(name, [P, words.shape[2]], I32)
@@ -83,22 +89,21 @@ def tile_list_parish_record_hints_kernel(
         nc.sync.dma_start(out=gain_t[:], in_=gain.rearrange("(b p t) -> p b t", b=NPASS, t=PACK))
         base_t = keep("base_t", [P, NPASS, PACK], F32)
         nc.sync.dma_start(out=base_t[:], in_=base.rearrange("(b p t) -> p b t", b=NPASS, t=PACK))
-
-        def load_w4(b):
-            raw = keep("w4_raw%d" % b, [P, NPASS * 2 * PASS], U8)
-            nc.sync.dma_start(
-                out=raw[:].bitcast(I32).rearrange("p (a c) -> p a c", a=NPASS),
-                in_=w4_words[:, :, 2 * PASS * b : 2 * PASS * (b + 1)].bitcast(I32).rearrange("a p c -> p a c"),
-            )
-            return raw
-
-        w4_raw = [load_w4(0)]
+        w4_w = keep("w4_w", [P, NPASS * 2 * H], U8)
+        nc.sync.dma_start(
+            out=w4_w[:].bitcast(I32).rearrange("p (a c) -> p a c", a=NPASS),
+            in_=w4_words.bitcast(I32).rearrange("a p c -> p a c"),
+        )
         tab_w = [load_words("words0", tab_words, 0)]
         load_planes(nc.sync, tab_s, tab_scales)
-        w1_raw = {(0, 0): load_w1(0, 0)}
-        load_planes(nc.sync, w4_s, w4_scales)
         tab_w.append(load_words("words1", tab_words, 1))
+        w1_raw = {(0, 0): load_w1(0, 0)}
         w1_raw[(0, 1)] = load_w1(0, 1)
+        for q in range(4):
+            nc.sync.dma_start(
+                out=tab2_s[32 * q : 32 * q + 4 * NPASS, :].bitcast(I32),
+                in_=tab2_scales[:, 4 * q : 4 * q + 4, :].bitcast(I32),
+            )
         wgs_t = keep("wgs_t", [P, PACK * S], F32)
 
         def load_wgs(lo, hi):
@@ -110,29 +115,13 @@ def tile_list_parish_record_hints_kernel(
 
         load_wgs(0, 2)
         pages = [load_page(0)]
-        w4_raw.append(load_w4(1))
-        pages.append(load_page(1))
         w1_raw[(1, 0)] = load_w1(1, 0)
-        load_wgs(2, PACK)
+        pages.append(load_page(1))
         w1_raw[(1, 1)] = load_w1(1, 1)
+        load_wgs(2, PACK)
         pages.append(load_page(2))
         pages.append(load_page(3))
-        for q in range(4):
-            nc.sync.dma_start(
-                out=tab2_s[32 * q : 32 * q + 4 * NPASS, :].bitcast(I32),
-                in_=tab2_scales[:, 4 * q : 4 * q + 4, :].bitcast(I32),
-            )
 
-        w4_w, w4_p = {}, {}
-
-        def deal_w4_words(b, tile):
-            w4_w[b] = tile
-            nc.vector.tensor_copy(
-                out=tile[:].bitcast(U16).rearrange("p (a t m) -> p a m t", t=PACK, m=P),
-                in_=w4_raw[b][:].bitcast(U16).rearrange("p (a m t) -> p a m t", t=PACK, m=P),
-            )
-
-        deal_w4_words(0, keep("w4_w0", [P, NPASS * 2 * PASS], U8))
         v_w, v_s = [], []
         for a in range(NPASS):
             words = keep("v_w%d" % a, [P, S], U32)
@@ -141,16 +130,7 @@ def tile_list_parish_record_hints_kernel(
             nc.vector.tensor_copy(plane[:], tab_s[:, T * a : T * (a + 1)].indirect(o1[:]))
             v_w.append(words)
             v_s.append(plane)
-
-        def deal_w4_planes(b, tile):
-            w4_p[b] = tile
-            nc.vector.tensor_copy(
-                out=tile[:].rearrange("p (a t m) -> p a m t", a=NPASS, t=PACK, m=P),
-                in_=w4_s[:].rearrange("p (a b m t) -> p b a m t", a=NPASS, t=PACK, m=P)[:, b],
-            )
-
-        deal_w4_planes(0, keep("w4_p0", [P, NPASS * PASS], U8))
-        tab2_w = [load_words("words%d" % a, tab2_words, a) for a in range(NPASS)]
+        tab2_w = {a: load_words("words%d" % a, tab2_words, a) for a in (1, 0)}
         for s in range(PACK, 2 * PACK):
             pages.append(load_page(s))
         minus_base = keep("minus_base", [P, NPASS, PACK], F32)
@@ -179,63 +159,84 @@ def tile_list_parish_record_hints_kernel(
                     in_=grouped[:, PACK * lo : PACK * hi],
                 )
 
-        work = [held.tile([P, 2, 2, S], F32, name="work%d" % u, align_bytes=64) for u in range(PACK)]
-        factor = {}
+        def place(name, shape, dtype, kib):
+            return shared.tile(shape, dtype, name=name, offset=1024 * kib, align_bytes=64)
 
-        def make_factor(s, place):
-            b, t = divmod(s, PACK)
-            factor[s] = place
-            nc.scalar.activation(
-                out=place, in_=wgs_t[:, S * t : S * (t + 1)], func=ACT.Copy, scale=gain_t[:, b, t : t + 1]
-            )
+        plus = [place("plus0", [P, PACK, PASS], F32, 8), keep("plus1", [P, PACK, PASS], F32)]
+        minus = [keep("minus%d" % b, [P, PACK, PASS], F32) for b in range(NPASS)]
 
-        def first_stage(s):
-            b, t = divmod(s, PACK)
-            u, h = divmod(s, 2)
-            swap = t // 2
-            acc_b = psum.tile([P, S], F32, name="bank%d" % (PACK * b + 2 * h + swap))
-            acc_a = psum.tile([P, S], F32, name="bank%d" % (PACK * b + 2 * h + 1 - swap))
-            for a in range(NPASS):
-                c0 = PASS * a + P * t
-                nc.tensor.matmul_mx(
-                    out=acc_b[:],
-                    lhsT=w4_w[b][:, 2 * c0 : 2 * (c0 + P)].bitcast(FP4X4),
-                    lhsT_scale=w4_p[b][:, c0 : c0 + P],
-                    rhs=v_w[a][:].bitcast(FP8X4), rhs_scale=v_s[a][:],
-                    start=(a == 0), stop=(a == NPASS - 1),
+        def w4_products(b):
+            for jt in range(PACK):
+                acc = psum.tile([P, PASS], F32, name="bank%d" % (PACK + jt))
+                for a in range(NPASS):
+                    c0 = H * a + PASS * b
+                    nc.tensor.matmul_mx(
+                        out=acc[:],
+                        lhsT=v_w[a][:, P * jt : P * (jt + 1)].bitcast(FP8X4),
+                        lhsT_scale=v_s[a][:, P * jt : P * (jt + 1)],
+                        rhs=w4_w[:, 2 * c0 : 2 * (c0 + PASS)].bitcast(FP4X4), rhs_scale=w4_s[:, c0 : c0 + PASS],
+                        start=(a == 0), stop=(a == NPASS - 1),
+                    )
+                nc.scalar.activation(
+                    out=minus[b][:, jt, :].rearrange("p (t m) -> p t m", t=PACK),
+                    in_=acc[:].rearrange("p (m t) -> p t m", t=PACK), func=ACT.Abs,
                 )
-            for a in range(NPASS):
-                nc.tensor.matmul_mx(
-                    out=acc_a[:],
-                    lhsT=w1_w[(b, a)][:, P * t : P * (t + 1)].bitcast(FP8X4),
-                    lhsT_scale=w1_s[(b, a)][:, P * t : P * (t + 1)],
-                    rhs=v_w[a][:].bitcast(FP8X4), rhs_scale=v_s[a][:],
-                    start=(a == 0), stop=(a == NPASS - 1),
-                )
-            nc.scalar.activation(out=work[u][:, h, 1, :], in_=acc_b[:], func=ACT.Abs)
-            nc.scalar.activation(out=work[u][:, h, 0, :], in_=acc_a[:], func=ACT.Abs)
+                if jt % 2:
+                    pair = minus[b][:, jt - 1 : jt + 1, :]
+                    if b == 0:
+                        nc.vector.tensor_scalar(pair, pair, -1.0, None, ALU.mult)
+                    else:
+                        nc.scalar.activation(out=pair, in_=pair, func=ACT.Copy, scale=-1.0)
 
-        for a, share, cuts in ((0, P, (0, PASS)), (1, 0, (0, P, PASS))):
-            fresh = shared.tile([P, PACK * PASS], BF16, name="grouped%d" % a, offset=2 * PACK * PASS * a, align_bytes=64)
-            weave_w1(0, a, share, fresh[:])
-            quantise_w1(0, a, cuts)
+        def w1_product(s):
+            b, t = divmod(s, PACK)
+            acc = psum.tile([P, S], F32, name="bank%d" % (2 * b + t % 2))
+            for a in range(NPASS):
+                for jt in range(PACK):
+                    nc.tensor.matmul_mx(
+                        out=acc[:, P * jt : P * (jt + 1)],
+                        lhsT=v_w[a][:, P * jt : P * (jt + 1)].bitcast(FP8X4),
+                        lhsT_scale=v_s[a][:, P * jt : P * (jt + 1)],
+                        rhs=w1_w[(b, a)][:, P * t : P * (t + 1)].bitcast(FP8X4),
+                        rhs_scale=w1_s[(b, a)][:, P * t : P * (t + 1)],
+                        start=(a == 0 and jt == 0), stop=(a == NPASS - 1 and jt == PACK - 1),
+                    )
+            nc.scalar.activation(out=plus[b][:, t, :], in_=acc[:], func=ACT.Abs)
+
+        turned, feature = {}, {}
+
+        def turn(s):
+            b, t = divmod(s, PACK)
+            acc = psum.tile([P, S], F32, name="bank%d" % (PACK + t))
+            turned[s] = acc
+            for jt in range(PACK):
+                cols = slice(P * jt, P * (jt + 1))
+                nc.tensor.matmul(
+                    acc[:, cols], minus[b][:, jt, P * t : P * (t + 1)], ident[:], start=True, stop=False, is_transpose=True
+                )
+                nc.tensor.matmul(acc[:, cols], plus[b][:, t, cols], ident[:], start=False, stop=True, is_transpose=True)
+
+        def scale_by_gain(s, tile):
+            b, t = divmod(s, PACK)
+            feature[s] = tile
+            nc.scalar.activation(out=tile[:], in_=turned[s][:], func=ACT.Copy, scale=gain_t[:, b, t : t + 1])
+
+        weave_w1(0, 0, 0, place("grouped00", [P, PACK * PASS], BF16, 0)[:])
+        quantise_w1(0, 0, (0, PASS))
+        weave_w1(0, 1, 0, place("grouped01", [P, PACK * PASS], BF16, 4)[:])
+        quantise_w1(0, 1, (0, P, PASS))
+        w4_products(0)
         for s in range(PACK):
-            first_stage(s)
-
-        deal_w4_words(1, shared.tile([P, NPASS * 2 * PASS], U8, name="w4_w1", offset=2 * PACK * PASS, align_bytes=64))
-        deal_w4_planes(1, shared.tile([P, NPASS * PASS], U8, name="w4_p1", offset=3 * PACK * PASS, align_bytes=64))
-
-        def as_bf16(pair):
-            return pair.rearrange("p h s -> p (h s)").bitcast(BF16)
+            w1_product(s)
+            turn(s)
+            if s < PACK - 1:
+                scale_by_gain(s, keep("feature%d" % s, [P, S], F32))
 
         x4, m4 = {}, {}
 
-        def subtract(u, part):
-            nc.vector.tensor_tensor(work[u][:, part, 0, :], work[u][:, part, 0, :], work[u][:, part, 1, :], ALU.subtract)
-
         def scatter(s):
-            u, h = divmod(s, 2)
-            nc.vector.tensor_tensor(pages[s][:].indirect(o3[:]), work[u][:, h, 0, :], factor[s], ALU.mult)
+            t = s % PACK
+            nc.vector.tensor_tensor(pages[s][:].indirect(o3[:]), feature[s][:], wgs_t[:, S * t : S * (t + 1)], ALU.mult)
 
         def fetch(s):
             b, t = divmod(s, PACK)
@@ -275,14 +276,12 @@ def tile_list_parish_record_hints_kernel(
             )
 
         half = S2 // 2
-        v2_s = keep("v2_s", [P, S2], U8)
         v2_w = {}
 
-        def gather_records(g, name):
+        def gather_records(g, a, tile):
+            v2_w[(g, a)] = tile
             part = o2[:, (half // 16) * g : (half // 16) * (g + 1)]
-            v2_w[g] = keep(name, [P, NPASS, half], U32)
-            for a in range(NPASS):
-                nc.vector.tensor_copy(v2_w[g][:, a, :], tab2_w[a][:].bitcast(U32).indirect(part))
+            nc.vector.tensor_copy(tile[:], tab2_w[a][:].bitcast(U32).indirect(part))
 
         accs = {}
 
@@ -298,69 +297,71 @@ def tile_list_parish_record_hints_kernel(
                 accs[(mt, e)] = psum.tile([P, PJ], F32, name="bank%d" % bank_of(mt, e))
             nc.tensor.matmul_mx(
                 out=accs[(mt, e)][:],
-                lhsT=v2_w[g][:, a, c0 : c0 + P].bitcast(FP8X4),
+                lhsT=v2_w[(g, a)][:, c0 : c0 + P].bitcast(FP8X4),
                 lhsT_scale=v2_s[4 * a : P, P * mt : P * (mt + 1)],
                 rhs=x_w[(e, a)][:].bitcast(FP8X4), rhs_scale=x_s[(e, a)][:],
                 start=(a == 0), stop=(a == NPASS - 1),
             )
 
         def copy_out(mt):
-            u, h = divmod(mt, 2)
-            nc.scalar.copy(out=work[u][:, h, 0, :], in_=accs[(mt, 1)][:])
+            nc.scalar.copy(out=minus[mt // PACK][:, mt % PACK, :], in_=accs[(mt, 1)][:])
 
         def finish(mt):
-            u, h = divmod(mt, 2)
-            nc.vector.tensor_tensor(work[u][:, h, 1, :], accs[(mt, 0)][:], work[u][:, h, 0, :], ALU.max)
-            nc.sync.dma_start(out=out[P * mt : P * (mt + 1), :], in_=work[u][:, h, 1, :])
+            score = ring.tile([P, PJ], F32, name="score")
+            nc.vector.tensor_tensor(score[:], accs[(mt, 0)][:], minus[mt // PACK][:, mt % PACK, :], ALU.max)
+            nc.sync.dma_start(out=out[P * mt : P * (mt + 1), :], in_=score[:])
 
-        subtract(0, slice(0, 1))
-        first_factors = keep("first_factors", [P, 2, S], F32)
-        make_factor(0, first_factors[:, 0, :])
-        make_factor(1, first_factors[:, 1, :])
+        v2_s = place("v2_s", [P, S2], U8, 4)
         scatter(0)
-        subtract(0, slice(1, 2))
-        weave_w1(1, 0, P, as_bf16(work[0][:, 0]))
-        scatter(1)
-        weave_w1(1, 1, P, as_bf16(work[0][:, 1]))
-        for u in range(PACK - 1):
-            if u > 0:
-                scatter(2 * u)
-                scatter(2 * u + 1)
-            subtract(u + 1, slice(0, 2))
-            make_factor(2 * u + 2, work[u + 1][:, 0, 1, :])
-            if u < PACK - 2:
-                make_factor(2 * u + 3, work[u + 1][:, 1, 1, :])
-            fetch(2 * u)
-            fetch(2 * u + 1)
-            if u == 0:
-                quantise_w1(1, 0, (0, PASS))
-                quantise_w1(1, 1, (0, PASS))
-                for s in range(PACK, 2 * PACK):
-                    first_stage(s)
-            floor_on_scalar(2 * u)
-            floor_on_scalar(2 * u + 1)
-            if u == 1:
-                weave(0, 0)
-                weave(1, 0)
-        scatter(6)
         nc.vector.tensor_copy(v2_s[:], tab2_s[:].indirect(o2[:]))
+        for a in range(NPASS):
+            weave_w1(1, a, P, place("grouped1%d" % a, [P, PACK * PASS], BF16, 8 + 4 * a)[:])
+        scatter(1)
+        fetch(0)
+        fetch(1)
+        scatter(2)
+        for a in range(NPASS):
+            quantise_w1(1, a, (0, PASS))
+        scale_by_gain(3, place("feature3", [P, S], F32, 12))
+        w4_products(1)
+        for s in range(PACK, 2 * PACK):
+            w1_product(s)
+            turn(s)
+            if s < 2 * PACK - 1:
+                scale_by_gain(s, keep("feature%d" % s, [P, S], F32))
+        scatter(3)
+        fetch(2)
+        fetch(3)
+        gather_records(0, 1, place("v2_w01", [P, half], U32, 14))
+        for s in range(PACK):
+            floor_on_scalar(s)
+        weave(0, 0)
+        weave(1, 0)
+        scatter(4)
+        scatter(5)
+        fetch(4)
+        fetch(5)
+        scatter(6)
         for e in range(2):
             quantise_x(e, 0)
-        make_factor(7, x_g[(1, 0)][:].rearrange("p j t -> p (j t)").bitcast(F32)[:, :S])
-        gather_records(0, "x_g00")
+        scale_by_gain(7, keep("x_g10", [P, S], F32))
+        floor_on_scalar(4)
+        floor_on_scalar(5)
+        scatter(7)
+        gather_records(1, 0, keep("x_g00", [P, half], U32))
+        gather_records(0, 0, keep("x_g10", [P, half], U32))
+        fetch(6)
+        fetch(7)
         for mt in range(PACK):
             for e in range(2):
                 second_stage(mt, e, 0)
-        scatter(7)
-        fetch(6)
-        fetch(7)
-        floor_on_scalar(6)
+        floor_on_vector(6)
         floor_on_vector(2 * PACK - 1)
         weave(0, 1)
         weave(1, 1, on_vector=True)
         quantise_x(1, 1)
         quantise_x(0, 1)
-        gather_records(1, "x_g11")
+        gather_records(1, 1, keep("x_g11", [P, half], U32))
         for e in (1, 0):
             for mt in range(PACK):
                 second_stage(mt, e, 1)

@@ -47,18 +47,16 @@ def tile_list_parish_record_hints_kernel(
         tab2_s = keep("tab2_s", [P, T3], U8)
         nc.vector.memset(tab_s[:].bitcast(I32), 0)
         nc.gpsimd.memset(w4_s[:].bitcast(I32), 0)
+        nc.gpsimd.memset(tab2_s[:].bitcast(I32), 0)
+        ident = keep("ident", [P, P], F32)
+        make_identity(nc, ident[:])
 
-        def load_planes(queue, tile, scales):
-            for q in range(4):
+        def load_planes(queue, tile, scales, quadrants):
+            for q in quadrants:
                 queue.dma_start(
                     out=tile[32 * q : 32 * q + 4, :].bitcast(I32).rearrange("r (a t) -> r a t", a=NPASS),
                     in_=scales[:, 4 * q : 4 * q + 4, :].bitcast(I32).rearrange("a r t -> r a t"),
                 )
-
-        load_planes(nc.gpsimd, w4_s, w4_scales)
-        nc.gpsimd.memset(tab2_s[:].bitcast(I32), 0)
-        ident = keep("ident", [P, P], F32)
-        make_identity(nc, ident[:])
 
         def load_words(name, words, a):
             tile = keep(name, [P, words.shape[2]], I32)
@@ -82,7 +80,6 @@ def tile_list_parish_record_hints_kernel(
             return page
 
         nc.sync.dma_start(o1[:], offs)
-        nc.sync.dma_start(o2[:], offs2)
         nc.sync.dma_start(o3[:], offs3)
         nc.sync.dma_start(o4[:], offs4)
         gain_t = keep("gain_t", [P, NPASS, PACK], F32)
@@ -94,11 +91,13 @@ def tile_list_parish_record_hints_kernel(
             out=w4_w[:].bitcast(I32).rearrange("p (a c) -> p a c", a=NPASS),
             in_=w4_words.bitcast(I32).rearrange("a p c -> p a c"),
         )
-        tab_w = [load_words("words0", tab_words, 0)]
-        load_planes(nc.sync, tab_s, tab_scales)
-        tab_w.append(load_words("words1", tab_words, 1))
+        tab_w = [load_words("words%d" % a, tab_words, a) for a in range(NPASS)]
+        load_planes(nc.scalar, tab_s, tab_scales, range(4))
         w1_raw = {(0, 0): load_w1(0, 0)}
+        load_planes(nc.scalar, w4_s, w4_scales, range(1))
         w1_raw[(0, 1)] = load_w1(0, 1)
+        nc.sync.dma_start(o2[:], offs2)
+        load_planes(nc.scalar, w4_s, w4_scales, range(1, 4))
         for q in range(4):
             nc.sync.dma_start(
                 out=tab2_s[32 * q : 32 * q + 4 * NPASS, :].bitcast(I32),
@@ -190,7 +189,7 @@ def tile_list_parish_record_hints_kernel(
 
         def w1_product(s):
             b, t = divmod(s, PACK)
-            acc = psum.tile([P, S], F32, name="bank%d" % (2 * b + t % 2))
+            acc = psum.tile([P, S], F32, name="bank%d" % (t % 2 if b == 0 else t))
             for a in range(NPASS):
                 for jt in range(PACK):
                     nc.tensor.matmul_mx(

@@ -166,7 +166,7 @@ def tile_list_parish_record_hints_kernel(
 
         def w4_products(b):
             for jt in range(PACK):
-                acc = psum.tile([P, PASS], F32, name="bank%d" % (PACK + jt))
+                acc = psum.tile([P, PASS], F32, name="bank%d" % (PACK + (jt + b) % PACK))
                 for a in range(NPASS):
                     c0 = H * a + PASS * b
                     nc.tensor.matmul_mx(
@@ -187,55 +187,76 @@ def tile_list_parish_record_hints_kernel(
                     else:
                         nc.scalar.activation(out=pair, in_=pair, func=ACT.Copy, scale=-1.0)
 
-        def w1_product(s):
+        def w1_product(s, blocks, bank):
             b, t = divmod(s, PACK)
-            acc = psum.tile([P, S], F32, name="bank%d" % (t % 2 if b == 0 else t))
+            acc = psum.tile([P, len(blocks), P], F32, name="bank%d" % bank)
             for a in range(NPASS):
-                for jt in range(PACK):
+                for n, jt in enumerate(blocks):
                     nc.tensor.matmul_mx(
-                        out=acc[:, P * jt : P * (jt + 1)],
+                        out=acc[:, n, :],
                         lhsT=v_w[a][:, P * jt : P * (jt + 1)].bitcast(FP8X4),
                         lhsT_scale=v_s[a][:, P * jt : P * (jt + 1)],
                         rhs=w1_w[(b, a)][:, P * t : P * (t + 1)].bitcast(FP8X4),
                         rhs_scale=w1_s[(b, a)][:, P * t : P * (t + 1)],
-                        start=(a == 0 and jt == 0), stop=(a == NPASS - 1 and jt == PACK - 1),
+                        start=(a == 0 and n == 0), stop=(a == NPASS - 1 and n == len(blocks) - 1),
                     )
-            nc.scalar.activation(out=plus[b][:, t, :], in_=acc[:], func=ACT.Abs)
+            nc.scalar.activation(
+                out=plus[b][:, t, P * blocks[0] : P * (blocks[-1] + 1)], in_=acc[:].rearrange("p n m -> p (n m)"),
+                func=ACT.Abs,
+            )
 
-        turned, feature = {}, {}
-
-        def turn(s):
+        def turn(s, blocks, bank):
             b, t = divmod(s, PACK)
-            acc = psum.tile([P, S], F32, name="bank%d" % (PACK + t))
-            turned[s] = acc
-            for jt in range(PACK):
-                cols = slice(P * jt, P * (jt + 1))
+            acc = psum.tile([P, len(blocks), P], F32, name="bank%d" % bank)
+            for n, jt in enumerate(blocks):
                 nc.tensor.matmul(
-                    acc[:, cols], minus[b][:, jt, P * t : P * (t + 1)], ident[:], start=True, stop=False, is_transpose=True
+                    acc[:, n, :], minus[b][:, jt, P * t : P * (t + 1)], ident[:],
+                    start=True, stop=False, is_transpose=True,
                 )
-                nc.tensor.matmul(acc[:, cols], plus[b][:, t, cols], ident[:], start=False, stop=True, is_transpose=True)
+                nc.tensor.matmul(
+                    acc[:, n, :], plus[b][:, t, P * jt : P * (jt + 1)], ident[:],
+                    start=False, stop=True, is_transpose=True,
+                )
+            return acc
 
-        def scale_by_gain(s, tile):
+        feature = {}
+
+        def scale_by_gain(s, acc, dst):
             b, t = divmod(s, PACK)
+            nc.scalar.activation(
+                out=dst, in_=acc[:].rearrange("p n m -> p (n m)"), func=ACT.Copy, scale=gain_t[:, b, t : t + 1]
+            )
+
+        def features(s, product_bank, turn_bank):
+            w1_product(s, range(PACK), product_bank)
+            return turn(s, range(PACK), turn_bank)
+
+        def features_out(s, acc, tile):
             feature[s] = tile
-            nc.scalar.activation(out=tile[:], in_=turned[s][:], func=ACT.Copy, scale=gain_t[:, b, t : t + 1])
+            scale_by_gain(s, acc, tile[:])
 
         weave_w1(0, 0, 0, place("grouped00", [P, PACK * PASS], BF16, 0)[:])
         quantise_w1(0, 0, (0, PASS))
         weave_w1(0, 1, 0, place("grouped01", [P, PACK * PASS], BF16, 4)[:])
         quantise_w1(0, 1, (0, P, PASS))
         w4_products(0)
-        for s in range(PACK):
-            w1_product(s)
-            turn(s)
-            if s < PACK - 1:
-                scale_by_gain(s, keep("feature%d" % s, [P, S], F32))
+        feature[0] = keep("feature0", [P, S], F32)
+        for h in range(2):
+            blocks = range(2 * h, 2 * h + 2)
+            w1_product(0, blocks, h)
+            scale_by_gain(0, turn(0, blocks, PACK + h), feature[0][:, S // 2 * h : S // 2 * (h + 1)])
+        for s in (1, 2):
+            features_out(s, features(s, s + 1, PACK + s + 1), keep("feature%d" % s, [P, S], F32))
+        held_back = features(3, 0, PACK)
 
         x4, m4 = {}, {}
 
-        def scatter(s):
+        def scatter(s, lo=0, hi=S):
             t = s % PACK
-            nc.vector.tensor_tensor(pages[s][:].indirect(o3[:]), feature[s][:], wgs_t[:, S * t : S * (t + 1)], ALU.mult)
+            nc.vector.tensor_tensor(
+                pages[s][:].indirect(o3[:, lo // 16 : hi // 16]), feature[s][:, lo:hi],
+                wgs_t[:, S * t + lo : S * t + hi], ALU.mult,
+            )
 
         def fetch(s):
             b, t = divmod(s, PACK)
@@ -311,7 +332,8 @@ def tile_list_parish_record_hints_kernel(
             nc.sync.dma_start(out=out[P * mt : P * (mt + 1), :], in_=score[:])
 
         v2_s = place("v2_s", [P, S2], U8, 4)
-        scatter(0)
+        scatter(0, 0, S // 2)
+        scatter(0, S // 2, S)
         nc.vector.tensor_copy(v2_s[:], tab2_s[:].indirect(o2[:]))
         for a in range(NPASS):
             weave_w1(1, a, P, place("grouped1%d" % a, [P, PACK * PASS], BF16, 8 + 4 * a)[:])
@@ -321,13 +343,11 @@ def tile_list_parish_record_hints_kernel(
         scatter(2)
         for a in range(NPASS):
             quantise_w1(1, a, (0, PASS))
-        scale_by_gain(3, place("feature3", [P, S], F32, 12))
+        features_out(3, held_back, place("feature3", [P, S], F32, 12))
         w4_products(1)
-        for s in range(PACK, 2 * PACK):
-            w1_product(s)
-            turn(s)
-            if s < 2 * PACK - 1:
-                scale_by_gain(s, keep("feature%d" % s, [P, S], F32))
+        for s in range(PACK, 2 * PACK - 1):
+            features_out(s, features(s, s - PACK, s), keep("feature%d" % s, [P, S], F32))
+        held_back = features(7, 3, 7)
         scatter(3)
         fetch(2)
         fetch(3)
@@ -343,7 +363,7 @@ def tile_list_parish_record_hints_kernel(
         scatter(6)
         for e in range(2):
             quantise_x(e, 0)
-        scale_by_gain(7, keep("x_g10", [P, S], F32))
+        features_out(7, held_back, keep("x_g10", [P, S], F32))
         floor_on_scalar(4)
         floor_on_scalar(5)
         scatter(7)

from contextlib import ExitStack

import concourse.mybir as mybir
from concourse.masks import make_identity

K, H, T, S, T2, S2, T3, PJ = 1024, 1024, 2048, 512, 1024, 1024, 2048, 512
FLOPS = 2 * 2 * K * H * S + 2 * 2 * H * S2 * PJ

F32 = mybir.dt.float32
BF16 = mybir.dt.bfloat16
I32 = mybir.dt.int32
U32 = mybir.dt.uint32
U16 = mybir.dt.uint16
U8 = mybir.dt.uint8
FP8X4 = mybir.dt.float8_e4m3fn_x4
FP4X4 = mybir.dt.float4_e2m1fn_x4
ALU = mybir.AluOpType
ACT = mybir.ActivationFunctionType

P = 128
PACK = 4
PASS = P * PACK
NPASS = 2


def tile_list_parish_record_hints_kernel(
    tc, tab_words, tab_scales, offs, tab2_words, tab2_scales, offs2, offs3, offs4,
    w1, w4_words, w4_scales, gain, wgs, page0, base, out,
):
    nc = tc.nc
    with ExitStack() as ctx:
        held = ctx.enter_context(tc.tile_pool(name="held", bufs=1))
        shared = ctx.enter_context(tc.tile_pool(name="shared", bufs=1))
        ring = ctx.enter_context(tc.tile_pool(name="ring", bufs=4))
        psum = ctx.enter_context(tc.psum_pool(name="psum", bufs=1))

        def keep(name, shape, dtype):
            return held.tile(shape, dtype, name=name, align_bytes=64)

        o1 = keep("o1", [P, S // 16], U16)
        o2 = keep("o2", [P, S2 // 16], U16)
        o3 = keep("o3", [P, S // 16], U16)
        o4 = keep("o4", [P, PJ // 16], U16)

        tab_s = keep("tab_s", [P, NPASS * T], U8)
        w4_s = keep("w4_s", [P, NPASS * H], U8)
        tab2_s = keep("tab2_s", [P, T3], U8)
        nc.vector.memset(tab_s[:].bitcast(I32), 0)
        nc.gpsimd.memset(w4_s[:].bitcast(I32), 0)
        nc.gpsimd.memset(tab2_s[:].bitcast(I32), 0)
        ident = keep("ident", [P, P], F32)
        make_identity(nc, ident[:])

        def load_planes(queue, tile, scales, quadrants):
            for q in quadrants:
                queue.dma_start(
                    out=tile[32 * q : 32 * q + 4, :].bitcast(I32).rearrange("r (a t) -> r a t", a=NPASS),
                    in_=scales[:, 4 * q : 4 * q + 4, :].bitcast(I32).rearrange("a r t -> r a t"),
                )

        def load_words(name, words, a):
            tile = keep(name, [P, words.shape[2]], I32)
            nc.sync.dma_start(out=tile[:], in_=words[a].rearrange("p t i -> p (t i)").bitcast(I32))
            return tile

        def load_w1(b, a):
            raw = keep("raw%d" % a if b == 1 else "wide%d" % a, [P, PACK, PASS], F32)
            nc.sync.dma_start(
                out=raw[:],
                in_=w1[PASS * a : PASS * (a + 1), PASS * b : PASS * (b + 1)].rearrange("(p i) c -> p i c", i=PACK),
            )
            return raw

        def load_page(s):
            b, t = divmod(s, PACK)
            page = keep("page%d" % s, [P, T2], F32)
            nc.sync.dma_start(
                out=page[:], in_=page0[PASS * b : PASS * (b + 1), :].rearrange("(p t) c -> p t c", t=PACK)[:, t, :]
            )
            return page

        nc.sync.dma_start(o1[:], offs)
        nc.sync.dma_start(o3[:], offs3)
        nc.sync.dma_start(o4[:], offs4)
        gain_t = keep("gain_t", [P, NPASS, PACK], F32)
        nc.sync.dma_start(out=gain_t[:], in_=gain.rearrange("(b p t) -> p b t", b=NPASS, t=PACK))
        base_t = keep("base_t", [P, NPASS, PACK], F32)
        nc.sync.dma_start(out=base_t[:], in_=base.rearrange("(b p t) -> p b t", b=NPASS, t=PACK))
        w4_w = keep("w4_w", [P, NPASS * 2 * H], U8)
        nc.sync.dma_start(
            out=w4_w[:].bitcast(I32).rearrange("p (a c) -> p a c", a=NPASS),
            in_=w4_words.bitcast(I32).rearrange("a p c -> p a c"),
        )
        tab_w = [load_words("words%d" % a, tab_words, a) for a in range(NPASS)]
        load_planes(nc.scalar, tab_s, tab_scales, range(4))
        w1_raw = {(0, 0): load_w1(0, 0)}
        load_planes(nc.scalar, w4_s, w4_scales, range(1))
        w1_raw[(0, 1)] = load_w1(0, 1)
        nc.sync.dma_start(o2[:], offs2)
        load_planes(nc.scalar, w4_s, w4_scales, range(1, 4))
        for q in range(4):
            nc.sync.dma_start(
                out=tab2_s[32 * q : 32 * q + 4 * NPASS, :].bitcast(I32),
                in_=tab2_scales[:, 4 * q : 4 * q + 4, :].bitcast(I32),
            )
        wgs_t = keep("wgs_t", [P, PACK * S], F32)

        def load_wgs(lo, hi):
            for q in range(4):
                nc.sync.dma_start(
                    out=wgs_t[32 * q : 32 * q + 32, S * lo : S * hi],
                    in_=wgs.rearrange("(q t) j -> q (t j)", t=PACK)[:, S * lo : S * hi],
                )

        load_wgs(0, 2)
        pages = [load_page(0)]
        w1_raw[(1, 0)] = load_w1(1, 0)
        pages.append(load_page(1))
        w1_raw[(1, 1)] = load_w1(1, 1)
        load_wgs(2, PACK)
        pages.append(load_page(2))
        pages.append(load_page(3))

        v_w, v_s = [], []
        for a in range(NPASS):
            words = keep("v_w%d" % a, [P, S], U32)
            plane = keep("v_s%d" % a, [P, S], U8)
            nc.vector.tensor_copy(words[:], tab_w[a][:].bitcast(U32).indirect(o1[:]))
            nc.vector.tensor_copy(plane[:], tab_s[:, T * a : T * (a + 1)].indirect(o1[:]))
            v_w.append(words)
            v_s.append(plane)
        tab2_w = {a: load_words("words%d" % a, tab2_words, a) for a in (1, 0)}
        for s in range(PACK, 2 * PACK):
            pages.append(load_page(s))
        minus_base = keep("minus_base", [P, NPASS, PACK], F32)
        nc.scalar.activation(out=minus_base[:], in_=base_t[:], func=ACT.Copy, scale=-1.0)

        w1_w, w1_s = {}, {}

        w1_g = {}

        def weave_w1(b, a, scalar_share, grouped):
            w1_g[(b, a)] = grouped
            dst = grouped.rearrange("p (t m i) -> p m i t", t=PACK, i=PACK)
            src = w1_raw[(b, a)][:].rearrange("p i (m t) -> p m i t", t=PACK)
            if scalar_share:
                nc.scalar.activation(out=dst, in_=src, func=ACT.Copy)
            else:
                nc.vector.tensor_copy(out=dst, in_=src)

        def quantise_w1(b, a, cuts):
            grouped = w1_g[(b, a)]
            w1_w[(b, a)] = keep("w1_w%d%d" % (b, a), [P, PASS], U32)
            w1_s[(b, a)] = keep("w1_s%d%d" % (b, a), [P, PASS], U8)
            for lo, hi in zip(cuts, cuts[1:]):
                nc.vector.quantize_mx(
                    out=w1_w[(b, a)][:, lo:hi].bitcast(FP8X4), scales=w1_s[(b, a)][:, lo:hi],
                    in_=grouped[:, PACK * lo : PACK * hi],
                )

        def place(name, shape, dtype, kib):
            return shared.tile(shape, dtype, name=name, offset=1024 * kib, align_bytes=64)

        plus = [place("plus0", [P, PACK, PASS], F32, 8), keep("plus1", [P, PACK, PASS], F32)]
        minus = [keep("minus%d" % b, [P, PACK, PASS], F32) for b in range(NPASS)]

        def w4_products(b):
            for jt in range(PACK):
                acc = psum.tile([P, PASS], F32, name="bank%d" % (PACK + (jt + b) % PACK))
                for a in range(NPASS):
                    c0 = H * a + PASS * b
                    nc.tensor.matmul_mx(
                        out=acc[:],
                        lhsT=v_w[a][:, P * jt : P * (jt + 1)].bitcast(FP8X4),
                        lhsT_scale=v_s[a][:, P * jt : P * (jt + 1)],
                        rhs=w4_w[:, 2 * c0 : 2 * (c0 + PASS)].bitcast(FP4X4), rhs_scale=w4_s[:, c0 : c0 + PASS],
                        start=(a == 0), stop=(a == NPASS - 1),
                    )
                nc.scalar.activation(
                    out=minus[b][:, jt, :].rearrange("p (t m) -> p t m", t=PACK),
                    in_=acc[:].rearrange("p (m t) -> p t m", t=PACK), func=ACT.Abs,
                )
                if jt % 2:
                    pair = minus[b][:, jt - 1 : jt + 1, :]
                    if b == 0:
                        nc.vector.tensor_scalar(pair, pair, -1.0, None, ALU.mult)
                    else:
                        nc.scalar.activation(out=pair, in_=pair, func=ACT.Copy, scale=-1.0)

        def w1_product(s, blocks, bank):
            b, t = divmod(s, PACK)
            acc = psum.tile([P, len(blocks), P], F32, name="bank%d" % bank)
            for a in range(NPASS):
                for n, jt in enumerate(blocks):
                    nc.tensor.matmul_mx(
                        out=acc[:, n, :],
                        lhsT=v_w[a][:, P * jt : P * (jt + 1)].bitcast(FP8X4),
                        lhsT_scale=v_s[a][:, P * jt : P * (jt + 1)],
                        rhs=w1_w[(b, a)][:, P * t : P * (t + 1)].bitcast(FP8X4),
                        rhs_scale=w1_s[(b, a)][:, P * t : P * (t + 1)],
                        start=(a == 0 and n == 0), stop=(a == NPASS - 1 and n == len(blocks) - 1),
                    )
            nc.scalar.activation(
                out=plus[b][:, t, P * blocks[0] : P * (blocks[-1] + 1)], in_=acc[:].rearrange("p n m -> p (n m)"),
                func=ACT.Abs,
            )

        def turn(s, blocks, bank):
            b, t = divmod(s, PACK)
            acc = psum.tile([P, len(blocks), P], F32, name="bank%d" % bank)
            for n, jt in enumerate(blocks):
                nc.tensor.matmul(
                    acc[:, n, :], minus[b][:, jt, P * t : P * (t + 1)], ident[:],
                    start=True, stop=False, is_transpose=True,
                )
                nc.tensor.matmul(
                    acc[:, n, :], plus[b][:, t, P * jt : P * (jt + 1)], ident[:],
                    start=False, stop=True, is_transpose=True,
                )
            return acc

        feature = {}

        def scale_by_gain(s, acc, dst):
            b, t = divmod(s, PACK)
            nc.scalar.activation(
                out=dst, in_=acc[:].rearrange("p n m -> p (n m)"), func=ACT.Copy, scale=gain_t[:, b, t : t + 1]
            )

        def features(s, product_bank, turn_bank):
            w1_product(s, range(PACK), product_bank)
            return turn(s, range(PACK), turn_bank)

        def features_out(s, acc, tile):
            feature[s] = tile
            scale_by_gain(s, acc, tile[:])

        weave_w1(0, 0, 0, place("grouped00", [P, PACK * PASS], BF16, 0)[:])
        quantise_w1(0, 0, (0, PASS))
        weave_w1(0, 1, 0, place("grouped01", [P, PACK * PASS], BF16, 4)[:])
        quantise_w1(0, 1, (0, P, PASS))
        w4_products(0)
        feature[0] = keep("feature0", [P, S], F32)
        for h in range(2):
            blocks = range(2 * h, 2 * h + 2)
            w1_product(0, blocks, h)
            scale_by_gain(0, turn(0, blocks, PACK + h), feature[0][:, S // 2 * h : S // 2 * (h + 1)])
        for s in (1, 2):
            features_out(s, features(s, s + 1, PACK + s + 1), keep("feature%d" % s, [P, S], F32))
        held_back = features(3, 0, PACK)

        x4, m4 = {}, {}

        def scatter(s, lo=0, hi=S):
            t = s % PACK
            nc.vector.tensor_tensor(
                pages[s][:].indirect(o3[:, lo // 16 : hi // 16]), feature[s][:, lo:hi],
                wgs_t[:, S * t + lo : S * t + hi], ALU.mult,
            )

        def fetch(s):
            b, t = divmod(s, PACK)
            if t == 0:
                x4[b] = keep("wide%d" % b, [P, PACK, PJ], F32)
                m4[b] = keep("raw%d" % (1 - b), [P, PACK, PJ], F32)
            nc.vector.tensor_copy(x4[b][:, t, :], pages[s][:].indirect(o4[:]))

        def floor_on_scalar(s):
            b, t = divmod(s, PACK)
            above = m4[b][:, t, :]
            nc.scalar.activation(out=above, in_=x4[b][:, t, :], func=ACT.Relu, bias=minus_base[:, b, t : t + 1])
            nc.scalar.activation(out=m4[b][:, t, :], in_=above, func=ACT.Identity, bias=base_t[:, b, t : t + 1])

        def floor_on_vector(s):
            b, t = divmod(s, PACK)
            nc.vector.tensor_scalar(m4[b][:, t, :], x4[b][:, t, :], base_t[:, b, t : t + 1], None, ALU.max)

        x_w, x_s, x_g = {}, {}, {}

        def weave(e, b, on_vector=False):
            grouped = keep("x_g%d%d" % (e, b), [P, PJ, PACK], BF16)
            dst = grouped[:].rearrange("p (c i) t -> p c t i", i=4)
            src = (x4, m4)[e][b][:].rearrange("p t (c i) -> p c t i", i=4)
            if on_vector:
                nc.vector.tensor_copy(out=dst, in_=src)
            else:
                nc.scalar.activation(out=dst, in_=src, func=(ACT.Abs, ACT.Copy)[e])
            x_g[(e, b)] = grouped

        def quantise_x(e, b):
            x_w[(e, b)] = keep("x_w%d%d" % (e, b), [P, PJ], U32)
            x_s[(e, b)] = keep("x_s%d%d" % (e, b), [P, PJ], U8)
            nc.vector.quantize_mx(
                out=x_w[(e, b)][:].bitcast(FP8X4), scales=x_s[(e, b)][:],
                in_=x_g[(e, b)][:].rearrange("p j t -> p (j t)"),
            )

        half = S2 // 2
        v2_w = {}

        def gather_records(g, a, tile):
            v2_w[(g, a)] = tile
            part = o2[:, (half // 16) * g : (half // 16) * (g + 1)]
            nc.vector.tensor_copy(tile[:], tab2_w[a][:].bitcast(U32).indirect(part))

        accs = {}

        def bank_of(mt, e):
            if mt < PACK:
                return 2 * mt + e
            late = 2 * (mt - PACK) + (1 - e)
            return 2 * (late % PACK) + (1 - late // PACK)

        def second_stage(mt, e, a):
            g, c0 = divmod(P * mt, half)
            if a == 0:
                accs[(mt, e)] = psum.tile([P, PJ], F32, name="bank%d" % bank_of(mt, e))
            nc.tensor.matmul_mx(
                out=accs[(mt, e)][:],
                lhsT=v2_w[(g, a)][:, c0 : c0 + P].bitcast(FP8X4),
                lhsT_scale=v2_s[4 * a : P, P * mt : P * (mt + 1)],
                rhs=x_w[(e, a)][:].bitcast(FP8X4), rhs_scale=x_s[(e, a)][:],
                start=(a == 0), stop=(a == NPASS - 1),
            )

        def copy_out(mt):
            nc.scalar.copy(out=minus[mt // PACK][:, mt % PACK, :], in_=accs[(mt, 1)][:])

        def finish(mt):
            score = ring.tile([P, PJ], F32, name="score")
            nc.vector.tensor_tensor(score[:], accs[(mt, 0)][:], minus[mt // PACK][:, mt % PACK, :], ALU.max)
            nc.sync.dma_start(out=out[P * mt : P * (mt + 1), :], in_=score[:])

        v2_s = place("v2_s", [P, S2], U8, 4)
        scatter(0, 0, S // 2)
        scatter(0, S // 2, S)
        nc.vector.tensor_copy(v2_s[:], tab2_s[:].indirect(o2[:]))
        for a in range(NPASS):
            weave_w1(1, a, P, place("grouped1%d" % a, [P, PACK * PASS], BF16, 8 + 4 * a)[:])
        scatter(1)
        fetch(0)
        fetch(1)
        scatter(2)
        for a in range(NPASS):
            quantise_w1(1, a, (0, PASS))
        features_out(3, held_back, place("feature3", [P, S], F32, 12))
        w4_products(1)
        for s in range(PACK, 2 * PACK - 1):
            features_out(s, features(s, s - PACK, s), keep("feature%d" % s, [P, S], F32))
        held_back = features(7, 3, 7)
        scatter(3)
        fetch(2)
        fetch(3)
        gather_records(0, 1, place("v2_w01", [P, half], U32, 14))
        for s in range(PACK):
            floor_on_scalar(s)
        weave(0, 0)
        weave(1, 0)
        scatter(4)
        scatter(5)
        fetch(4)
        fetch(5)
        scatter(6)
        for e in range(2):
            quantise_x(e, 0)
        features_out(7, held_back, keep("x_g10", [P, S], F32))
        floor_on_scalar(4)
        floor_on_scalar(5)
        scatter(7)
        gather_records(1, 0, keep("x_g00", [P, half], U32))
        gather_records(0, 0, keep("x_g10", [P, half], U32))
        fetch(6)
        fetch(7)
        for mt in range(PACK):
            for e in range(2):
                second_stage(mt, e, 0)
        floor_on_vector(6)
        floor_on_vector(2 * PACK - 1)
        weave(0, 1)
        weave(1, 1, on_vector=True)
        quantise_x(1, 1)
        quantise_x(0, 1)
        gather_records(1, 1, keep("x_g11", [P, half], U32))
        for e in (1, 0):
            for mt in range(PACK):
                second_stage(mt, e, 1)
        for mt in range(PACK):
            copy_out(mt)
        for mt in range(PACK):
            finish(mt)
        for mt in range(PACK, 2 * PACK):
            for e in (1, 0):
                for a in range(NPASS):
                    second_stage(mt, e, a)
            copy_out(mt)
            finish(mt)
